import numpy as np
import ml_dtypes

BF16 = ml_dtypes.bfloat16


def bf(x):
    return np.asarray(x, np.float32).astype(BF16)


def f32(x):
    return np.asarray(x, np.float32)


def f64(x):
    return np.asarray(x).astype(np.float64)


def striped(idx):
    return np.concatenate([l.reshape(-1, 16).T for l in idx])


def rows(idx, k):
    return np.tile(np.repeat(idx, 16, axis=0), (k // (16 * 8), 1))


def look(tab, idx):
    return np.take_along_axis(f64(tab), rows(idx, len(tab)), axis=1)


K, S, V, N, M = 512, 2048, 1536, 1536, 256


def setup_inputs():
    return {"tab": f32(np.random.standard_normal((K, S))), "s": f32(np.random.uniform(0.5, 1.5, (K, 1))), "c": f32(0.3 * np.random.standard_normal((K, 1))), "w": bf(np.random.standard_normal((K, M)) / np.sqrt(K)), "offs": striped(np.random.randint(0, S, (8, N)))}


def reference(tab, s, c, w, offs):
    idx = np.stack([g.T.reshape(-1) for g in np.split(offs, 8)])
    t = look(tab, idx)
    x = f64(s) * t + f64(c)
    y = f64(w).T @ x
    return y

@@ -1,0 +1,75 @@
+import concourse.mybir as mybir
+
+ROWS, COLUMNS, LIST, OUT_ROWS = 512, 2048, 1536, 256
+P = 128
+BLOCKS = ROWS // P
+PIECE = 512
+PIECES = LIST // PIECE
+HALVES = OUT_ROWS // P
+PIECE_COLUMNS = PIECE // 16
+
+FLOPS = 2 * ROWS * LIST * OUT_ROWS
+
+F32, BF16, U16 = mybir.dt.float32, mybir.dt.bfloat16, mybir.dt.uint16
+MULT, ADD = mybir.AluOpType.mult, mybir.AluOpType.add
+
+
+def tile_lookup_deq_affp_none_kernel(tc, tab, s, c, w, offs, out):
+    nc = tc.nc
+    with (
+        tc.tile_pool(name="held", bufs=1) as held,
+        tc.tile_pool(name="work", bufs=3) as work,
+        tc.psum_pool(name="psum", bufs=1) as psum,
+    ):
+        lists = held.tile([P, LIST // 16], U16, name="lists")
+        nc.sync.dma_start(lists[:], offs)
+
+        scale = held.tile([P, BLOCKS], F32, name="scale")
+        shift = held.tile([P, BLOCKS], F32, name="shift")
+        weights = held.tile([P, BLOCKS, OUT_ROWS], BF16, name="weights")
+        with nc.allow_non_contiguous_dma(reason="one float32 for each row"):
+            nc.scalar.dma_start(scale[:], s.rearrange("(b p) o -> p (b o)", p=P))
+            nc.scalar.dma_start(shift[:], c.rearrange("(b p) o -> p (b o)", p=P))
+        nc.scalar.dma_start(weights[:], w.rearrange("(b p) m -> p b m", p=P))
+
+        windows = []
+        for b in range(BLOCKS):
+            window = held.tile([P, COLUMNS], F32, name=f"window{b}")
+            nc.sync.dma_start(window[:], tab[b * P : (b + 1) * P, :])
+            windows.append(window)
+
+        sums = [
+            [psum.tile([P, PIECE], F32, name=f"sum{p}_{h}") for h in range(HALVES)]
+            for p in range(PIECES)
+        ]
+
+        for b in range(BLOCKS):
+            for p in range(PIECES):
+                piece = lists[:, p * PIECE_COLUMNS : (p + 1) * PIECE_COLUMNS]
+                x = work.tile([P, PIECE], F32, name="x")
+                nc.vector.tensor_scalar(
+                    x[:],
+                    windows[b][:].indirect(piece),
+                    scale[:, b : b + 1],
+                    shift[:, b : b + 1],
+                    MULT,
+                    ADD,
+                )
+                x_rounded = work.tile([P, PIECE], BF16, name="x_rounded")
+                nc.scalar.copy(x_rounded[:], x[:])
+                for h in range(HALVES):
+                    nc.tensor.matmul(
+                        sums[p][h][:],
+                        weights[:, b, h * P : (h + 1) * P],
+                        x_rounded[:],
+                        start=b == 0,
+                        stop=b == BLOCKS - 1,
+                    )
+
+        for p in range(PIECES):
+            for h in range(HALVES):
+                staged = work.tile([P, PIECE], F32, name="staged")
+                nc.scalar.copy(staged[:], sums[p][h][:])
+                nc.sync.dma_start(
+                    out[h * P : (h + 1) * P, p * PIECE : (p + 1) * PIECE], staged[:]
+                )

@@ -1,4 +1,5 @@
 import concourse.mybir as mybir
+from concourse.masks import make_identity
 
 ROWS, COLUMNS, LIST, OUT_ROWS = 512, 2048, 1536, 256
 P = 128
@@ -6,6 +7,7 @@ BLOCKS = ROWS // P
 PIECE = 512
 PIECES = LIST // PIECE
 HALVES = OUT_ROWS // P
+ROW_TILE = 64
 PIECE_COLUMNS = PIECE // 16
 
 FLOPS = 2 * ROWS * LIST * OUT_ROWS
@@ -24,19 +26,26 @@ def tile_lookup_deq_affp_none_kernel(tc, tab, s, c, w, offs, out):
         lists = held.tile([P, LIST // 16], U16, name="lists")
         nc.sync.dma_start(lists[:], offs)
 
-        scale = held.tile([P, BLOCKS], F32, name="scale")
-        shift = held.tile([P, BLOCKS], F32, name="shift")
-        weights = held.tile([P, BLOCKS, OUT_ROWS], BF16, name="weights")
-        with nc.allow_non_contiguous_dma(reason="one float32 for each row"):
-            nc.scalar.dma_start(scale[:], s.rearrange("(b p) o -> p (b o)", p=P))
-            nc.scalar.dma_start(shift[:], c.rearrange("(b p) o -> p (b o)", p=P))
-        nc.scalar.dma_start(weights[:], w.rearrange("(b p) m -> p b m", p=P))
+        rows = held.tile([ROW_TILE, P], F32, name="rows")
+        nc.gpsimd.memset(rows[:], 0.0)
+        nc.scalar.dma_start(rows[:BLOCKS, :], s.rearrange("(b p) o -> b (p o)", p=P))
+        nc.scalar.dma_start(rows[BLOCKS : 2 * BLOCKS, :], c.rearrange("(b p) o -> b (p o)", p=P))
 
         windows = []
+        weights = held.tile([P, BLOCKS, OUT_ROWS], BF16, name="weights")
         for b in range(BLOCKS):
             window = held.tile([P, COLUMNS], F32, name=f"window{b}")
             nc.sync.dma_start(window[:], tab[b * P : (b + 1) * P, :])
             windows.append(window)
+            if b == 0:
+                nc.sync.dma_start(weights[:], w.rearrange("(b p) m -> p b m", p=P))
+
+        identity = held.tile([ROW_TILE, ROW_TILE], F32, name="identity")
+        make_identity(nc, identity[:])
+        turned = psum.tile([P, ROW_TILE], F32, name="turned")
+        nc.tensor.transpose(turned[:], rows[:], identity[:])
+        scale_shift = held.tile([P, 2 * BLOCKS], F32, name="scale_shift")
+        nc.vector.tensor_copy(scale_shift[:], turned[:, : 2 * BLOCKS])
 
         sums = [
             [psum.tile([P, PIECE], F32, name=f"sum{p}_{h}") for h in range(HALVES)]
@@ -50,8 +59,8 @@ def tile_lookup_deq_affp_none_kernel(tc, tab, s, c, w, offs, out):
                 nc.vector.tensor_scalar(
                     x[:],
                     windows[b][:].indirect(piece),
-                    scale[:, b : b + 1],
-                    shift[:, b : b + 1],
+                    scale_shift[:, b : b + 1],
+                    scale_shift[:, BLOCKS + b : BLOCKS + b + 1],
                     MULT,
                     ADD,
                 )

@@ -10,10 +10,17 @@ HALVES = OUT_ROWS // P
 ROW_TILE = 64
 PIECE_COLUMNS = PIECE // 16
 
+EARLY_BLOCKS = range(BLOCKS // 2)
+LATE_BLOCKS = range(BLOCKS // 2, BLOCKS)
+
 FLOPS = 2 * ROWS * LIST * OUT_ROWS
 
 F32, BF16, U16 = mybir.dt.float32, mybir.dt.bfloat16, mybir.dt.uint16
 MULT, ADD = mybir.AluOpType.mult, mybir.AluOpType.add
+
+
+def strips(p):
+    return [PIECE // 2, PIECE // 2] if p == PIECES - 1 else [PIECE]
 
 
 def tile_lookup_deq_affp_none_kernel(tc, tab, s, c, w, offs, out):
@@ -23,13 +30,13 @@ def tile_lookup_deq_affp_none_kernel(tc, tab, s, c, w, offs, out):
         tc.tile_pool(name="work", bufs=3) as work,
         tc.psum_pool(name="psum", bufs=1) as psum,
     ):
-        lists = held.tile([P, LIST // 16], U16, name="lists")
-        nc.sync.dma_start(lists[:], offs)
-
         rows = held.tile([ROW_TILE, P], F32, name="rows")
         nc.gpsimd.memset(rows[:], 0.0)
-        nc.scalar.dma_start(rows[:BLOCKS, :], s.rearrange("(b p) o -> b (p o)", p=P))
-        nc.scalar.dma_start(rows[BLOCKS : 2 * BLOCKS, :], c.rearrange("(b p) o -> b (p o)", p=P))
+        nc.sync.dma_start(rows[:BLOCKS, :], s.rearrange("(b p) o -> b (p o)", p=P))
+        nc.sync.dma_start(rows[BLOCKS : 2 * BLOCKS, :], c.rearrange("(b p) o -> b (p o)", p=P))
+
+        lists = held.tile([P, LIST // 16], U16, name="lists")
+        nc.sync.dma_start(lists[:], offs)
 
         windows = []
         weights = held.tile([P, BLOCKS, OUT_ROWS], BF16, name="weights")
@@ -42,33 +49,39 @@ def tile_lookup_deq_affp_none_kernel(tc, tab, s, c, w, offs, out):
 
         identity = held.tile([ROW_TILE, ROW_TILE], F32, name="identity")
         make_identity(nc, identity[:])
-        turned = psum.tile([P, ROW_TILE], F32, name="turned")
+        turned = psum.tile([P, ROW_TILE], F32, name="turned", tag="bank0_0_0")
         nc.tensor.transpose(turned[:], rows[:], identity[:])
         scale_shift = held.tile([P, 2 * BLOCKS], F32, name="scale_shift")
         nc.vector.tensor_copy(scale_shift[:], turned[:, : 2 * BLOCKS])
 
         sums = [
-            [psum.tile([P, PIECE], F32, name=f"sum{p}_{h}") for h in range(HALVES)]
+            [
+                [psum.tile([P, width], F32, name=f"sum{p}_{k}_{h}", tag=f"bank{p}_{k}_{h}") for h in range(HALVES)]
+                for k, width in enumerate(strips(p))
+            ]
             for p in range(PIECES)
         ]
 
-        for b in range(BLOCKS):
-            for p in range(PIECES):
-                piece = lists[:, p * PIECE_COLUMNS : (p + 1) * PIECE_COLUMNS]
-                x = work.tile([P, PIECE], F32, name="x")
-                nc.vector.tensor_scalar(
-                    x[:],
-                    windows[b][:].indirect(piece),
-                    scale_shift[:, b : b + 1],
-                    scale_shift[:, BLOCKS + b : BLOCKS + b + 1],
-                    MULT,
-                    ADD,
-                )
-                x_rounded = work.tile([P, PIECE], BF16, name="x_rounded")
-                nc.scalar.copy(x_rounded[:], x[:])
+        steps = [(b, p) for b in EARLY_BLOCKS for p in range(PIECES)]
+        steps += [(b, p) for p in range(PIECES) for b in LATE_BLOCKS]
+        for b, p in steps:
+            piece = lists[:, p * PIECE_COLUMNS : (p + 1) * PIECE_COLUMNS]
+            x = work.tile([P, PIECE], F32, name="x")
+            nc.vector.tensor_scalar(
+                x[:],
+                windows[b][:].indirect(piece),
+                scale_shift[:, b : b + 1],
+                scale_shift[:, BLOCKS + b : BLOCKS + b + 1],
+                MULT,
+                ADD,
+            )
+            for k, width in enumerate(strips(p)):
+                x_rounded = work.tile([P, width], BF16, name=f"x_rounded{width}")
+                cast = nc.vector.tensor_copy if (b, p) == steps[-1] else nc.scalar.copy
+                cast(x_rounded[:], x[:, k * width : (k + 1) * width])
                 for h in range(HALVES):
                     nc.tensor.matmul(
-                        sums[p][h][:],
+                        sums[p][k][h][:],
                         weights[:, b, h * P : (h + 1) * P],
                         x_rounded[:],
                         start=b == 0,
@@ -76,9 +89,10 @@ def tile_lookup_deq_affp_none_kernel(tc, tab, s, c, w, offs, out):
                     )
 
         for p in range(PIECES):
-            for h in range(HALVES):
-                staged = work.tile([P, PIECE], F32, name="staged")
-                nc.scalar.copy(staged[:], sums[p][h][:])
-                nc.sync.dma_start(
-                    out[h * P : (h + 1) * P, p * PIECE : (p + 1) * PIECE], staged[:]
-                )
+            for k, width in enumerate(strips(p)):
+                left = p * PIECE + k * width
+                for h in range(HALVES):
+                    staged = work.tile([P, width], F32, name=f"staged{width}", bufs=4)
+                    copy = nc.vector.tensor_copy if p == PIECES - 1 and h == 1 else nc.scalar.copy
+                    copy(staged[:], sums[p][k][h][:])
+                    nc.sync.dma_start(out[h * P : (h + 1) * P, left : left + width], staged[:])

import concourse.mybir as mybir
from concourse.masks import make_identity

ROWS, COLUMNS, LIST, OUT_ROWS = 512, 2048, 1536, 256
P = 128
BLOCKS = ROWS // P
PIECE = 512
PIECES = LIST // PIECE
HALVES = OUT_ROWS // P
ROW_TILE = 64
PIECE_COLUMNS = PIECE // 16

EARLY_BLOCKS = range(BLOCKS // 2)
LATE_BLOCKS = range(BLOCKS // 2, BLOCKS)

FLOPS = 2 * ROWS * LIST * OUT_ROWS

F32, BF16, U16 = mybir.dt.float32, mybir.dt.bfloat16, mybir.dt.uint16
MULT, ADD = mybir.AluOpType.mult, mybir.AluOpType.add


def strips(p):
    return [PIECE // 2, PIECE // 2] if p == PIECES - 1 else [PIECE]


def tile_lookup_deq_affp_none_kernel(tc, tab, s, c, w, offs, out):
    nc = tc.nc
    with (
        tc.tile_pool(name="held", bufs=1) as held,
        tc.tile_pool(name="work", bufs=3) as work,
        tc.psum_pool(name="psum", bufs=1) as psum,
    ):
        rows = held.tile([ROW_TILE, P], F32, name="rows")
        nc.gpsimd.memset(rows[:], 0.0)
        nc.sync.dma_start(rows[:BLOCKS, :], s.rearrange("(b p) o -> b (p o)", p=P))
        nc.sync.dma_start(rows[BLOCKS : 2 * BLOCKS, :], c.rearrange("(b p) o -> b (p o)", p=P))

        lists = held.tile([P, LIST // 16], U16, name="lists")
        nc.sync.dma_start(lists[:], offs)

        windows = []
        weights = held.tile([P, BLOCKS, OUT_ROWS], BF16, name="weights")
        for b in range(BLOCKS):
            window = held.tile([P, COLUMNS], F32, name=f"window{b}")
            nc.sync.dma_start(window[:], tab[b * P : (b + 1) * P, :])
            windows.append(window)
            if b == 0:
                nc.sync.dma_start(weights[:], w.rearrange("(b p) m -> p b m", p=P))

        identity = held.tile([ROW_TILE, ROW_TILE], F32, name="identity")
        make_identity(nc, identity[:])
        turned = psum.tile([P, ROW_TILE], F32, name="turned", tag="bank0_0_0")
        nc.tensor.transpose(turned[:], rows[:], identity[:])
        scale_shift = held.tile([P, 2 * BLOCKS], F32, name="scale_shift")
        nc.vector.tensor_copy(scale_shift[:], turned[:, : 2 * BLOCKS])

        sums = [
            [
                [psum.tile([P, width], F32, name=f"sum{p}_{k}_{h}", tag=f"bank{p}_{k}_{h}") for h in range(HALVES)]
                for k, width in enumerate(strips(p))
            ]
            for p in range(PIECES)
        ]

        steps = [(b, p) for b in EARLY_BLOCKS for p in range(PIECES)]
        steps += [(b, p) for p in range(PIECES) for b in LATE_BLOCKS]
        for b, p in steps:
            piece = lists[:, p * PIECE_COLUMNS : (p + 1) * PIECE_COLUMNS]
            x = work.tile([P, PIECE], F32, name="x")
            nc.vector.tensor_scalar(
                x[:],
                windows[b][:].indirect(piece),
                scale_shift[:, b : b + 1],
                scale_shift[:, BLOCKS + b : BLOCKS + b + 1],
                MULT,
                ADD,
            )
            for k, width in enumerate(strips(p)):
                x_rounded = work.tile([P, width], BF16, name=f"x_rounded{width}")
                cast = nc.vector.tensor_copy if (b, p) == steps[-1] else nc.scalar.copy
                cast(x_rounded[:], x[:, k * width : (k + 1) * width])
                for h in range(HALVES):
                    nc.tensor.matmul(
                        sums[p][k][h][:],
                        weights[:, b, h * P : (h + 1) * P],
                        x_rounded[:],
                        start=b == 0,
                        stop=b == BLOCKS - 1,
                    )

        for p in range(PIECES):
            for k, width in enumerate(strips(p)):
                left = p * PIECE + k * width
                for h in range(HALVES):
                    staged = work.tile([P, width], F32, name=f"staged{width}", bufs=4)
                    copy = nc.vector.tensor_copy if p == PIECES - 1 and h == 1 else nc.scalar.copy
                    copy(staged[:], sums[p][k][h][:])
                    nc.sync.dma_start(out[h * P : (h + 1) * P, left : left + width], staged[:])
